import numpy as np
import ml_dtypes


def mxq(x, axis, fmt="e4m3"):
    dtype, down = {"e4m3": (ml_dtypes.float8_e4m3fn, 7), "e5m2": (ml_dtypes.float8_e5m2, 14)}[fmt]
    v = np.moveaxis(np.asarray(x, np.float32).astype(ml_dtypes.bfloat16).astype(np.float64), axis, -1)
    blocks = v.reshape(v.shape[:-1] + (-1, 32))
    amax = np.abs(blocks).max(-1, keepdims=True)
    byte = np.maximum(np.where(amax > 0, np.frexp(amax)[1] - 1 + 127, 0) - down, 1)
    scale = np.exp2(byte - 127.0)
    codes = (blocks / scale).astype(np.float32).astype(dtype).astype(np.float64)
    return np.moveaxis((codes * scale).reshape(v.shape), -1, axis)


WIDE = False


def mx_kscale(k):
    if not WIDE:
        return np.ones(k)
    levels = np.array([10, -10, 5, -5, 0])
    if k % 512:
        return np.exp2(np.random.permutation(np.resize(levels, k // 32))).repeat(32)
    a = np.empty((k // 512, 16))
    for p in range(k // 512):
        a[p, :8] = np.random.permutation(np.resize(levels, 8))
        for g in range(8):
            far = levels[np.abs(levels - a[p, g]) >= 10]
            a[p, g + 8] = far[np.random.randint(len(far))]
    return np.exp2(a.ravel()).repeat(32)


def f64(x):
    return np.asarray(x).astype(np.float64)


def striped(idx):
    return np.tile(idx.reshape(-1, 16).T, (8, 1)).astype(np.uint16)


def unstriped(offs):
    return offs[:16].T.reshape(-1).astype(np.int64)


def striped8(idx):
    return np.concatenate([x.reshape(-1, 16).T for x in idx]).astype(np.uint16)


def runs(offs, k):
    lists = np.stack([offs[16 * r : 16 * r + 16].T.reshape(-1) for r in range(8)]).astype(np.int64)
    return lists[np.arange(k) % 512 // 64]


def pack_weight(w):
    k, n = w.shape
    w = f64(np.asarray(w, np.float32).astype(ml_dtypes.bfloat16)).reshape(k // 32, 32, n)
    amax = np.abs(w).max(1)
    byte = np.clip(np.where(amax > 0, np.frexp(amax)[1] - 1 + 127 - 7, 1), 1, 254)
    scaled = (w * np.exp2(127.0 - byte)[:, None, :]).reshape(k, n).astype(np.float32)
    words = np.ascontiguousarray(scaled.reshape(k // 512, 128, 4, n).transpose(0, 1, 3, 2)).astype(ml_dtypes.float8_e4m3fn).view(np.uint8)
    return words, np.ascontiguousarray(byte.astype(np.uint8).reshape(k // 512, 16, n))


def unpack_weight(words, scales):
    g, p, n, _ = words.shape
    vals = np.ascontiguousarray(words).view(ml_dtypes.float8_e4m3fn).astype(np.float64) * np.repeat(np.exp2(scales.astype(np.float64) - 127.0), 8, axis=1)[..., None]
    return vals.transpose(0, 1, 3, 2).reshape(g * 512, n)


K, T, S, H, C = 512, 2048, 512, 512, 512


def setup_inputs():
    n = np.random.standard_normal
    s = mx_kscale(K)[:, None]
    packed_xT = pack_weight(n((K, T)) * s)
    return {
        "x_words": packed_xT[0],
        "x_scales": packed_xT[1],
        "w1": (n((K, H)) / np.sqrt(K) / s).astype(np.float32),
        "gs": (np.random.uniform(0.5, 1.5, (K, 1)) / s).astype(np.float32),
        "offs": striped(np.random.permutation(T)[:S]),
        "n1": striped(np.random.permutation(S)),
        "n2": striped(np.random.permutation(S)),
        "ca": striped(np.random.permutation(T)[:C]),
        "cb": striped(np.random.permutation(T)[:C]),
        "n3": striped8(np.stack([np.random.permutation(S) for _ in range(8)])),
        "n4": striped8(np.stack([np.random.permutation(S) for _ in range(8)])),
    }


def reference(x_words, x_scales, w1, gs, offs, n1, n2, ca, cb, n3, n4):
    x_ca = unpack_weight(x_words, x_scales)[:, unstriped(ca)]
    xq = unpack_weight(x_words, x_scales)[:, unstriped(offs)]
    y = mxq(f64(w1), 0, "e4m3").T @ xq
    z = f64(gs) * (y[:, unstriped(n1)] / (np.abs(y) + np.abs(y[:, unstriped(n2)]) + 0.5))
    zq = mxq(z, 0, "e4m3")
    a = 0.0625 * (x_ca.T @ zq)
    x_cb = unpack_weight(x_words, x_scales)[:, unstriped(cb)]
    b = 0.0625 * (x_cb.T @ zq)
    return a[np.arange(C)[:, None], runs(n3, C)] - (np.tanh(b) * (b[np.arange(C)[:, None], runs(n4, C)]))

@@ -1,0 +1,294 @@
+from contextlib import ExitStack
+
+import concourse.mybir as mybir
+
+K, T, S, H, C = 512, 2048, 512, 512, 512
+FLOPS = 2 * K * H * S + 2 * 2 * K * C * S
+
+F32 = mybir.dt.float32
+BF16 = mybir.dt.bfloat16
+I32 = mybir.dt.int32
+U32 = mybir.dt.uint32
+U16 = mybir.dt.uint16
+U8 = mybir.dt.uint8
+FP8X4 = mybir.dt.float8_e4m3fn_x4
+ALU = mybir.AluOpType
+ACT = mybir.ActivationFunctionType
+
+P = 128
+PACK = 4
+HALF = S // 2
+LIST_COLS = S // 16
+ABS_ON_VECTOR = []
+
+
+def tile_picked_ccmpsoftbnorm2_none_p_kernel(
+    tc, x_words, x_scales, w1, gs, offs, n1, n2, ca, cb, n3, n4, out
+):
+    nc = tc.nc
+    with ExitStack() as ctx:
+        lists = ctx.enter_context(tc.tile_pool(name="lists", bufs=1))
+        keep = ctx.enter_context(tc.tile_pool(name="keep", bufs=1))
+        psum = ctx.enter_context(tc.psum_pool(name="psum", bufs=1))
+
+        def load_list(name, source):
+            tile = lists.tile([P, LIST_COLS], U16, name=name)
+            nc.sync.dma_start(tile[:], source)
+            return tile
+
+        def list_half(tile, h):
+            return tile[:, h * LIST_COLS // 2 : (h + 1) * LIST_COLS // 2]
+
+        def half(h):
+            return slice(h * HALF, (h + 1) * HALF)
+
+        def block(t):
+            return slice(t * P, (t + 1) * P)
+
+        def bank(index, shape):
+            return psum.tile(shape, F32, name="bank%d" % index)
+
+        def sbuf(name, shape, dtype, tag=None):
+            return keep.tile(shape, dtype, name=name, tag=tag or name, align_bytes=64)
+
+        def multiply(acc, lhs_words, lhs_scales, rhs_words, rhs_scales):
+            nc.tensor.matmul_mx(
+                out=acc,
+                lhsT=lhs_words.bitcast(FP8X4),
+                lhsT_scale=lhs_scales,
+                rhs=rhs_words.bitcast(FP8X4),
+                rhs_scale=rhs_scales,
+                start=True,
+                stop=True,
+            )
+
+        table_scales = sbuf("table_scales", [P, T], U8)
+        nc.vector.memset(table_scales[:].bitcast(I32), 0)
+        for q in range(4):
+            nc.scalar.dma_start(
+                table_scales[32 * q : 32 * q + 4, :].bitcast(I32),
+                x_scales[0, 4 * q : 4 * q + 4, :].bitcast(I32),
+            )
+        offs_list = load_list("offs_list", offs)
+        cb_list = load_list("cb_list", cb)
+        w_rows = w1.rearrange("(p j) c -> p j c", j=PACK)
+        w_raw = []
+        for h in range(2):
+            piece = sbuf("w_raw%d" % h, [P, PACK, H // 2], F32)
+            nc.sync.dma_start(piece[:], w_rows[:, :, h * H // 2 : (h + 1) * H // 2])
+            w_raw.append(piece)
+        table_words = sbuf("table_words", [P, T], U32)
+        nc.sync.dma_start(
+            table_words[:].bitcast(I32), x_words[0].rearrange("p n r -> p (n r)").bitcast(I32)
+        )
+        n2_list = load_list("n2_list", n2)
+        n1_list = load_list("n1_list", n1)
+        ca_list = load_list("ca_list", ca)
+        n4_list = load_list("n4_list", n4)
+        n3_list = load_list("n3_list", n3)
+        gain = sbuf("gain", [P, PACK], F32)
+        nc.gpsimd.dma_start(gain[:], gs.rearrange("(p t) o -> p (t o)", t=PACK))
+
+        def gather_scales(name, picks, tag):
+            tile = sbuf(name, [P, S], U8, tag)
+            nc.vector.tensor_copy(tile[:], table_scales[:].indirect(picks[:]))
+            return tile
+
+        def gather_words(name, picks, tag):
+            tile = sbuf(name, [P, S], U32, tag)
+            nc.vector.tensor_copy(tile[:], table_words[:].indirect(picks[:]))
+            return tile
+
+        def deal(name, picked, dtype, run, tag):
+            tile = sbuf(name, [P, C], dtype, tag)
+            dst = tile[:].bitcast(I32) if dtype == U32 else tile[:]
+            src = picked.bitcast(I32) if dtype == U32 else picked
+            nc.vector.tensor_copy(
+                dst.rearrange("p (t c i) -> p c t i", t=PACK, i=run),
+                src.rearrange("p (c i t) -> p c t i", t=PACK, i=run),
+            )
+            return tile
+
+        token_scales = gather_scales("token_scales", offs_list, "token_scales")
+        cb_scales_picked = gather_scales("cb_scales_picked", cb_list, "cb_scales_picked")
+
+        w_bf = sbuf("w_bf", [P, PACK, P, PACK], BF16)
+        w_dst = w_bf[:].rearrange("p t m j -> p m t j")
+        for h in range(2):
+            nc.scalar.copy(
+                w_dst[:, h * P // 2 : (h + 1) * P // 2], w_raw[h][:].rearrange("p j (m t) -> p m t j", t=PACK)
+            )
+        w_words = sbuf("w_words", [P, H], U32)
+        w_scales = sbuf("w_scales", [P, H], U8)
+        nc.vector.quantize_mx(
+            out=w_words[:].bitcast(FP8X4), scales=w_scales[:], in_=w_bf[:].rearrange("p t m j -> p (t m j)")
+        )
+        early_words = sbuf("early_words", [P, 2, S], U32, "w_bf")
+        token_words = early_words[:, 0]
+        cb_words_picked = early_words[:, 1]
+        for h in range(2):
+            nc.vector.tensor_copy(token_words[:, half(h)], table_words[:].indirect(list_half(offs_list, h)))
+        y_psum = [bank(t, [P, S]) for t in range(PACK)]
+        for u in range(2):
+            for h, t in [(0, 2 * u), (0, 2 * u + 1), (1, 2 * u), (1, 2 * u + 1)]:
+                multiply(
+                    y_psum[t][:, half(h)],
+                    w_words[:, block(t)],
+                    w_scales[:, block(t)],
+                    token_words[:, half(h)],
+                    token_scales[:, half(h)],
+                )
+        nc.vector.tensor_copy(cb_words_picked, table_words[:].indirect(cb_list[:]))
+
+        y_rows = [sbuf("y_rows%d" % t, [P, S], F32) for t in range(PACK)]
+        y_size = [sbuf("y_size%d" % t, [P, S], F32) for t in range(PACK)]
+        upper, other, denom, root, part = {}, {}, {}, {}, {}
+        z_words = sbuf("z_words", [P, S], U32)
+        z_scales = sbuf("z_scales", [P, S], U8)
+
+        def open_half(h):
+            upper[h] = sbuf("upper%d" % h, [P, PACK, HALF], F32, "upper")
+            other[h] = sbuf("other%d" % h, [P, PACK, HALF], F32, "other")
+            denom[h] = sbuf("denom%d" % h, [P, PACK, HALF], F32)
+            root[h] = sbuf("root%d" % h, [P, PACK, HALF], F32)
+            part[h] = sbuf("part%d" % h, [P, PACK, HALF], F32)
+
+        def leave_psum(t):
+            if t in ABS_ON_VECTOR:
+                nc.vector.tensor_copy(y_rows[t][:], y_psum[t][:])
+                nc.vector.scalar_tensor_tensor(y_size[t][:], y_psum[t][:], -1.0, y_rows[t][:], ALU.mult, ALU.max)
+            else:
+                nc.scalar.activation(y_size[t][:], y_psum[t][:], ACT.Abs)
+                nc.vector.tensor_copy(y_rows[t][:], y_psum[t][:])
+
+        def fetch_upper(h, t):
+            nc.scalar.activation(upper[h][:, t], y_rows[t][:].indirect(list_half(n1_list, h)), ACT.Copy)
+
+        def fetch_other(h, t):
+            nc.scalar.activation(other[h][:, t], y_size[t][:].indirect(list_half(n2_list, h)), ACT.Copy)
+            nc.vector.scalar_tensor_tensor(
+                denom[h][:, t], other[h][:, t], 0.5, y_size[t][:, half(h)], ALU.add, ALU.add
+            )
+
+        def take_root(h, t):
+            nc.scalar.activation(root[h][:, t], denom[h][:, t], ACT.Abs_reciprocal_sqrt)
+
+        def first_product(h, t):
+            nc.vector.scalar_tensor_tensor(
+                part[h][:, t], upper[h][:, t], gain[:, t : t + 1], root[h][:, t], ALU.mult, ALU.mult
+            )
+
+        def quantise_z(h):
+            z_bf = sbuf("z_bf%d" % h, [P, HALF * PACK], BF16)
+            nc.vector.tensor_tensor(
+                z_bf[:].rearrange("p (c i t) -> p c t i", i=2, t=PACK),
+                part[h][:].rearrange("p t (c i) -> p c t i", i=2),
+                root[h][:].rearrange("p t (c i) -> p c t i", i=2),
+                ALU.mult,
+            )
+            nc.vector.quantize_mx(out=z_words[:, half(h)].bitcast(FP8X4), scales=z_scales[:, half(h)], in_=z_bf[:])
+
+        b_psum = {}
+
+        def score_b(h):
+            for u in range(2):
+                acc = bank(4 + 2 * h + u, [P, 2, HALF])
+                for e in range(2):
+                    t = 2 * u + e
+                    multiply(
+                        acc[:, e],
+                        cb_words[:, block(t)],
+                        cb_scales[:, block(t)],
+                        z_words[:, half(h)],
+                        z_scales[:, half(h)],
+                    )
+                    b_psum[(h, t)] = acc[:, e]
+
+        open_half(0)
+        leave_psum(0)
+        leave_psum(1)
+        fetch_other(0, 0)
+        fetch_upper(0, 0)
+        take_root(0, 0)
+        first_product(0, 0)
+        leave_psum(2)
+        fetch_other(0, 1)
+        fetch_upper(0, 1)
+        take_root(0, 1)
+        first_product(0, 1)
+        cb_words = deal("cb_words", cb_words_picked, U32, 4, "w_words")
+        cb_scales = deal("cb_scales", cb_scales_picked[:], U8, 16, "w_scales")
+        leave_psum(3)
+        fetch_other(0, 2)
+        fetch_upper(0, 2)
+        take_root(0, 2)
+        first_product(0, 2)
+        fetch_other(0, 3)
+        fetch_upper(0, 3)
+        take_root(0, 3)
+        first_product(0, 3)
+        ca_scales_picked = gather_scales("ca_scales_picked", ca_list, "token_scales")
+        ca_scales = deal("ca_scales", ca_scales_picked[:], U8, 16, "ca_scales")
+
+        quantise_z(0)
+        score_b(0)
+
+        open_half(1)
+        fetch_other(1, 0)
+        fetch_other(1, 1)
+        take_root(1, 0)
+        fetch_upper(1, 0)
+        first_product(1, 0)
+        ca_words_picked = gather_words("ca_words_picked", ca_list, "z_bf0")
+        ca_words = deal("ca_words", ca_words_picked[:], U32, 4, "ca_words")
+        fetch_other(1, 2)
+        take_root(1, 1)
+        fetch_upper(1, 1)
+        first_product(1, 1)
+        fetch_other(1, 3)
+        take_root(1, 2)
+        fetch_upper(1, 2)
+        first_product(1, 2)
+        take_root(1, 3)
+        fetch_upper(1, 3)
+        first_product(1, 3)
+
+        quantise_z(1)
+        score_b(1)
+
+        a_psum = [bank(t, [P, S]) for t in range(PACK)]
+        for t in range(PACK):
+            multiply(a_psum[t][:], ca_words[:, block(t)], ca_scales[:, block(t)], z_words[:], z_scales[:])
+
+        spent = ["denom1", "upper", "part1", "root1"]
+        b_window = [sbuf("b_window%d" % t, [P, 2 * S], F32, spent[t]) for t in range(PACK)]
+        a_window = [sbuf("a_window%d" % t, [P, 2 * S], F32) for t in range(PACK)]
+        for h in range(2):
+            for t in range(PACK):
+                nc.scalar.activation(
+                    b_window[t][:, S + h * HALF : S + (h + 1) * HALF], b_psum[(h, t)], ACT.Tanh, scale=0.0625
+                )
+        for t in range(PACK):
+            for h in range(2):
+                nc.vector.tensor_copy(b_window[t][:, half(h)], b_psum[(h, t)])
+            nc.vector.tensor_copy(a_window[t][:, 0:S], a_psum[t][:])
+
+        out_rows = out.rearrange("(p t) j -> t p j", t=PACK)
+        for t in range(PACK):
+            nc.scalar.activation(a_window[t][:, S : 2 * S], b_window[t][:].indirect(n4_list[:]), ACT.Copy)
+            gated = sbuf("gated%d" % t, [P, S], F32)
+            nc.vector.scalar_tensor_tensor(
+                gated[:], a_window[t][:, S : 2 * S], 0.0625, b_window[t][:, S : 2 * S], ALU.mult, ALU.mult
+            )
+            a_picked = sbuf("a_picked%d" % t, [P, S], F32)
+            result = sbuf("result%d" % t, [P, S], F32)
+            pieces = 2 if t == PACK - 1 else 1
+            width = S // pieces
+            for piece in range(pieces):
+                cols = slice(piece * width, (piece + 1) * width)
+                picks = n3_list[:, piece * width // 16 : (piece + 1) * width // 16]
+                nc.scalar.activation(a_picked[:, cols], a_window[t][:].indirect(picks), ACT.Copy)
+                nc.vector.scalar_tensor_tensor(
+                    result[:, cols], a_picked[:, cols], 0.0625, gated[:, cols], ALU.mult, ALU.subtract
+                )
+                nc.sync.dma_start(out_rows[t][:, cols], result[:, cols])

@@ -19,7 +19,7 @@ P = 128
 PACK = 4
 HALF = S // 2
 LIST_COLS = S // 16
-ABS_ON_VECTOR = []
+SPARE = 8
 
 
 def tile_picked_ccmpsoftbnorm2_none_p_kernel(
@@ -69,6 +69,9 @@ def tile_picked_ccmpsoftbnorm2_none_p_kernel(
                 table_scales[32 * q : 32 * q + 4, :].bitcast(I32),
                 x_scales[0, 4 * q : 4 * q + 4, :].bitcast(I32),
             )
+        warm = sbuf("warm", [P, 16], F32)
+        nc.vector.memset(warm[:, 0:8], 1.0)
+        nc.scalar.activation(warm[:, 8:16], warm[:, 0:8], ACT.Abs_reciprocal_sqrt)
         offs_list = load_list("offs_list", offs)
         cb_list = load_list("cb_list", cb)
         w_rows = w1.rearrange("(p j) c -> p j c", j=PACK)
@@ -140,155 +143,195 @@ def tile_picked_ccmpsoftbnorm2_none_p_kernel(
                 )
         nc.vector.tensor_copy(cb_words_picked, table_words[:].indirect(cb_list[:]))
 
-        y_rows = [sbuf("y_rows%d" % t, [P, S], F32) for t in range(PACK)]
-        y_size = [sbuf("y_size%d" % t, [P, S], F32) for t in range(PACK)]
-        upper, other, denom, root, part = {}, {}, {}, {}, {}
+        y_rows = [sbuf("y_rows%d" % t, [P, S + SPARE], F32) for t in range(PACK)]
+        y_size = [sbuf("y_size%d" % t, [P, S + SPARE], F32) for t in range(PACK)]
+        for t in range(PACK):
+            nc.gpsimd.memset(y_rows[t][:, S : S + SPARE], 0.0)
+            nc.gpsimd.memset(y_size[t][:, S : S + SPARE], 0.0)
+        root = sbuf("root", [P, 2, PACK, HALF], F32)
+        part = sbuf("part", [P, 2, PACK, HALF], F32)
         z_words = sbuf("z_words", [P, S], U32)
         z_scales = sbuf("z_scales", [P, S], U8)
+        denom = {}
 
-        def open_half(h):
-            upper[h] = sbuf("upper%d" % h, [P, PACK, HALF], F32, "upper")
-            other[h] = sbuf("other%d" % h, [P, PACK, HALF], F32, "other")
-            denom[h] = sbuf("denom%d" % h, [P, PACK, HALF], F32)
-            root[h] = sbuf("root%d" % h, [P, PACK, HALF], F32)
-            part[h] = sbuf("part%d" % h, [P, PACK, HALF], F32)
+        upper = {}
+        other = {}
 
-        def leave_psum(t):
-            if t in ABS_ON_VECTOR:
-                nc.vector.tensor_copy(y_rows[t][:], y_psum[t][:])
-                nc.vector.scalar_tensor_tensor(y_size[t][:], y_psum[t][:], -1.0, y_rows[t][:], ALU.mult, ALU.max)
-            else:
-                nc.scalar.activation(y_size[t][:], y_psum[t][:], ACT.Abs)
-                nc.vector.tensor_copy(y_rows[t][:], y_psum[t][:])
+        def span(h0, h1):
+            return slice(h0 * HALF, h1 * HALF)
 
-        def fetch_upper(h, t):
-            nc.scalar.activation(upper[h][:, t], y_rows[t][:].indirect(list_half(n1_list, h)), ACT.Copy)
+        def picks_of(tile, h0, h1):
+            return tile[:, h0 * HALF // 16 : h1 * HALF // 16]
 
-        def fetch_other(h, t):
-            nc.scalar.activation(other[h][:, t], y_size[t][:].indirect(list_half(n2_list, h)), ACT.Copy)
+        def copy_y(t):
+            nc.vector.tensor_copy(y_rows[t][:, 0:S], y_psum[t][:])
+
+        def size_on_scalar(t):
+            nc.scalar.activation(y_size[t][:, 0:S], y_psum[t][:], ACT.Abs)
+
+        def size_on_vector(t):
+            nc.vector.scalar_tensor_tensor(y_size[t][:, 0:S], y_psum[t][:], -1.0, y_rows[t][:, 0:S], ALU.mult, ALU.max)
+
+        def fetch_other(t, h0, h1, tag=None):
+            other[(t, h0)] = sbuf("other%d_%d" % (t, h0), [P, (h1 - h0) * HALF], F32, tag)
+            nc.scalar.activation(other[(t, h0)][:], y_size[t][:].indirect(picks_of(n2_list, h0, h1)), ACT.Copy)
+
+        def fetch_upper(t, h0, h1, tag=None):
+            upper[(t, h0)] = sbuf("upper%d_%d" % (t, h0), [P, (h1 - h0) * HALF], F32, tag)
+            nc.scalar.activation(upper[(t, h0)][:], y_rows[t][:].indirect(picks_of(n1_list, h0, h1)), ACT.Copy)
+
+        def add_sizes(t, h0, h1):
+            denom[(t, h0)] = sbuf("denom%d_%d" % (t, h0), [P, (h1 - h0) * HALF], F32)
             nc.vector.scalar_tensor_tensor(
-                denom[h][:, t], other[h][:, t], 0.5, y_size[t][:, half(h)], ALU.add, ALU.add
+                denom[(t, h0)][:], other[(t, h0)][:], 0.5, y_size[t][:, span(h0, h1)], ALU.add, ALU.add
             )
 
-        def take_root(h, t):
-            nc.scalar.activation(root[h][:, t], denom[h][:, t], ACT.Abs_reciprocal_sqrt)
-
-        def first_product(h, t):
-            nc.vector.scalar_tensor_tensor(
-                part[h][:, t], upper[h][:, t], gain[:, t : t + 1], root[h][:, t], ALU.mult, ALU.mult
+        def take_root(t, h0, h1):
+            nc.scalar.activation(
+                root[:, h0:h1, t], denom[(t, h0)][:].rearrange("p (h c) -> p h c", c=HALF), ACT.Abs_reciprocal_sqrt
             )
 
-        def quantise_z(h):
+        def first_product(t, h0, h1):
+            nc.vector.scalar_tensor_tensor(
+                part[:, h0:h1, t],
+                upper[(t, h0)][:].rearrange("p (h c) -> p h c", c=HALF),
+                gain[:, t : t + 1],
+                root[:, h0:h1, t],
+                ALU.mult,
+                ALU.mult,
+            )
+
+        z_planes = {}
+
+        def second_product(h):
             z_bf = sbuf("z_bf%d" % h, [P, HALF * PACK], BF16)
             nc.vector.tensor_tensor(
                 z_bf[:].rearrange("p (c i t) -> p c t i", i=2, t=PACK),
-                part[h][:].rearrange("p t (c i) -> p c t i", i=2),
-                root[h][:].rearrange("p t (c i) -> p c t i", i=2),
+                part[:, h].rearrange("p t (c i) -> p c t i", i=2),
+                root[:, h].rearrange("p t (c i) -> p c t i", i=2),
                 ALU.mult,
             )
-            nc.vector.quantize_mx(out=z_words[:, half(h)].bitcast(FP8X4), scales=z_scales[:, half(h)], in_=z_bf[:])
+            z_planes[h] = z_bf
 
-        b_psum = {}
+        def quantise_z(h):
+            nc.vector.quantize_mx(
+                out=z_words[:, half(h)].bitcast(FP8X4), scales=z_scales[:, half(h)], in_=z_planes[h][:]
+            )
+
+        b_psum = [bank(PACK + t, [P, S]) for t in range(PACK)]
 
         def score_b(h):
-            for u in range(2):
-                acc = bank(4 + 2 * h + u, [P, 2, HALF])
-                for e in range(2):
-                    t = 2 * u + e
-                    multiply(
-                        acc[:, e],
-                        cb_words[:, block(t)],
-                        cb_scales[:, block(t)],
-                        z_words[:, half(h)],
-                        z_scales[:, half(h)],
-                    )
-                    b_psum[(h, t)] = acc[:, e]
+            for t in range(PACK):
+                multiply(
+                    b_psum[t][:, half(h)],
+                    cb_words[:, block(t)],
+                    cb_scales[:, block(t)],
+                    z_words[:, half(h)],
+                    z_scales[:, half(h)],
+                )
 
-        open_half(0)
-        leave_psum(0)
-        leave_psum(1)
-        fetch_other(0, 0)
-        fetch_upper(0, 0)
-        take_root(0, 0)
-        first_product(0, 0)
-        leave_psum(2)
-        fetch_other(0, 1)
-        fetch_upper(0, 1)
-        take_root(0, 1)
-        first_product(0, 1)
+        size_on_scalar(0)
+        copy_y(0)
+        copy_y(1)
+        copy_y(2)
+        size_on_vector(1)
+        copy_y(3)
+        size_on_vector(2)
+        size_on_vector(3)
+        fetch_other(0, 0, 2)
+        fetch_upper(0, 0, 2)
+        fetch_other(1, 0, 2)
+        fetch_upper(1, 0, 2)
+        fetch_other(2, 0, 1)
+        fetch_other(3, 0, 1)
+        fetch_upper(2, 0, 1)
+        fetch_upper(3, 0, 1)
         cb_words = deal("cb_words", cb_words_picked, U32, 4, "w_words")
         cb_scales = deal("cb_scales", cb_scales_picked[:], U8, 16, "w_scales")
-        leave_psum(3)
-        fetch_other(0, 2)
-        fetch_upper(0, 2)
-        take_root(0, 2)
-        first_product(0, 2)
-        fetch_other(0, 3)
-        fetch_upper(0, 3)
-        take_root(0, 3)
-        first_product(0, 3)
         ca_scales_picked = gather_scales("ca_scales_picked", ca_list, "token_scales")
+        add_sizes(0, 0, 2)
+        add_sizes(1, 0, 2)
+        add_sizes(2, 0, 1)
+        add_sizes(3, 0, 1)
         ca_scales = deal("ca_scales", ca_scales_picked[:], U8, 16, "ca_scales")
-
+        take_root(0, 0, 2)
+        first_product(0, 0, 2)
+        take_root(1, 0, 2)
+        first_product(1, 0, 2)
+        take_root(2, 0, 1)
+        first_product(2, 0, 1)
+        take_root(3, 0, 1)
+        first_product(3, 0, 1)
+        second_product(0)
+        fetch_other(2, 1, 2, "denom2_0")
+        fetch_other(3, 1, 2, "denom3_0")
+        add_sizes(2, 1, 2)
+        add_sizes(3, 1, 2)
         quantise_z(0)
         score_b(0)
-
-        open_half(1)
-        fetch_other(1, 0)
-        fetch_other(1, 1)
-        take_root(1, 0)
-        fetch_upper(1, 0)
-        first_product(1, 0)
-        ca_words_picked = gather_words("ca_words_picked", ca_list, "z_bf0")
-        ca_words = deal("ca_words", ca_words_picked[:], U32, 4, "ca_words")
-        fetch_other(1, 2)
-        take_root(1, 1)
-        fetch_upper(1, 1)
-        first_product(1, 1)
-        fetch_other(1, 3)
-        take_root(1, 2)
-        fetch_upper(1, 2)
-        first_product(1, 2)
-        take_root(1, 3)
-        fetch_upper(1, 3)
-        first_product(1, 3)
-
+        fetch_upper(2, 1, 2, "upper2_0")
+        take_root(2, 1, 2)
+        take_root(3, 1, 2)
+        fetch_upper(3, 1, 2, "upper3_0")
+        first_product(2, 1, 2)
+        first_product(3, 1, 2)
+        second_product(1)
         quantise_z(1)
-        score_b(1)
 
-        a_psum = [bank(t, [P, S]) for t in range(PACK)]
-        for t in range(PACK):
-            multiply(a_psum[t][:], ca_words[:, block(t)], ca_scales[:, block(t)], z_words[:], z_scales[:])
-
-        spent = ["denom1", "upper", "part1", "root1"]
+        spent = ["denom3_1","upper3_0","part","root"]
         b_window = [sbuf("b_window%d" % t, [P, 2 * S], F32, spent[t]) for t in range(PACK)]
         a_window = [sbuf("a_window%d" % t, [P, 2 * S], F32) for t in range(PACK)]
-        for h in range(2):
+        gated = {}
+        a_psum = {}
+        out_rows = out.rearrange("(p t) j -> t p j", t=PACK)
+
+        def take_tanh(h):
             for t in range(PACK):
                 nc.scalar.activation(
-                    b_window[t][:, S + h * HALF : S + (h + 1) * HALF], b_psum[(h, t)], ACT.Tanh, scale=0.0625
+                    b_window[t][:, S + h * HALF : S + (h + 1) * HALF], b_psum[t][:, half(h)], ACT.Tanh, scale=0.0625
                 )
-        for t in range(PACK):
-            for h in range(2):
-                nc.vector.tensor_copy(b_window[t][:, half(h)], b_psum[(h, t)])
-            nc.vector.tensor_copy(a_window[t][:, 0:S], a_psum[t][:])
 
-        out_rows = out.rearrange("(p t) j -> t p j", t=PACK)
-        for t in range(PACK):
+        def copy_b(t):
+            nc.vector.tensor_scalar(b_window[t][:, 0:S], b_psum[t][:], 0.0625, None, ALU.mult)
+
+        def fetch_b(t):
             nc.scalar.activation(a_window[t][:, S : 2 * S], b_window[t][:].indirect(n4_list[:]), ACT.Copy)
-            gated = sbuf("gated%d" % t, [P, S], F32)
-            nc.vector.scalar_tensor_tensor(
-                gated[:], a_window[t][:, S : 2 * S], 0.0625, b_window[t][:, S : 2 * S], ALU.mult, ALU.mult
-            )
+
+        def score_a():
+            for t in range(PACK):
+                a_psum[t] = bank(t, [P, S])
+                multiply(a_psum[t][:], ca_words[:, block(t)], ca_scales[:, block(t)], z_words[:], z_scales[:])
+
+        def copy_a(t):
+            nc.vector.tensor_scalar(a_window[t][:, 0:S], a_psum[t][:], 0.0625, None, ALU.mult)
+
+        def apply_gate(t):
+            gated[t] = sbuf("gated%d" % t, [P, S], F32)
+            nc.vector.tensor_tensor(gated[t][:], a_window[t][:, S : 2 * S], b_window[t][:, S : 2 * S], ALU.mult)
+
+        def finish(t, pieces):
             a_picked = sbuf("a_picked%d" % t, [P, S], F32)
             result = sbuf("result%d" % t, [P, S], F32)
-            pieces = 2 if t == PACK - 1 else 1
             width = S // pieces
             for piece in range(pieces):
                 cols = slice(piece * width, (piece + 1) * width)
                 picks = n3_list[:, piece * width // 16 : (piece + 1) * width // 16]
                 nc.scalar.activation(a_picked[:, cols], a_window[t][:].indirect(picks), ACT.Copy)
-                nc.vector.scalar_tensor_tensor(
-                    result[:, cols], a_picked[:, cols], 0.0625, gated[:, cols], ALU.mult, ALU.subtract
-                )
+                nc.vector.tensor_tensor(result[:, cols], a_picked[:, cols], gated[t][:, cols], ALU.subtract)
                 nc.sync.dma_start(out_rows[t][:, cols], result[:, cols])
+
+        take_tanh(0)
+        score_b(1)
+        take_tanh(1)
+        ca_words_picked = gather_words("ca_words_picked", ca_list, "z_bf1")
+        ca_words = deal("ca_words", ca_words_picked[:], U32, 4, "w_words")
+        for t in range(PACK):
+            copy_b(t)
+            fetch_b(t)
+        score_a()
+        for t in range(PACK):
+            copy_a(t)
+        for t in range(PACK):
+            apply_gate(t)
+        for t in range(PACK):
+            finish(t, 2 if t == PACK - 1 else 1)

@@ -17,9 +17,13 @@ ACT = mybir.ActivationFunctionType
 
 P = 128
 PACK = 4
+GROUP = 16
+QUADRANTS = 4
 HALF = S // 2
-LIST_COLS = S // 16
 SPARE = 8
+SCORE_SCALE = 0.0625
+WHOLE_TILES = (0, 1)
+SPLIT_TILES = (2, 3)
 
 
 def tile_picked_ccmpsoftbnorm2_none_p_kernel(
@@ -31,25 +35,28 @@ def tile_picked_ccmpsoftbnorm2_none_p_kernel(
         keep = ctx.enter_context(tc.tile_pool(name="keep", bufs=1))
         psum = ctx.enter_context(tc.psum_pool(name="psum", bufs=1))
 
-        def load_list(name, source):
-            tile = lists.tile([P, LIST_COLS], U16, name=name)
-            nc.sync.dma_start(tile[:], source)
-            return tile
-
-        def list_half(tile, h):
-            return tile[:, h * LIST_COLS // 2 : (h + 1) * LIST_COLS // 2]
+        def halves(h0, h1):
+            return slice(h0 * HALF, h1 * HALF)
 
         def half(h):
-            return slice(h * HALF, (h + 1) * HALF)
+            return halves(h, h + 1)
+
+        def entries(list_tile, cols):
+            return list_tile[:, cols.start // GROUP : cols.stop // GROUP]
 
         def block(t):
             return slice(t * P, (t + 1) * P)
 
-        def bank(index, shape):
-            return psum.tile(shape, F32, name="bank%d" % index)
+        def bank(index, width):
+            return psum.tile([P, width], F32, name="bank%d" % index)
 
-        def sbuf(name, shape, dtype, tag=None):
-            return keep.tile(shape, dtype, name=name, tag=tag or name, align_bytes=64)
+        def sbuf(name, shape, dtype, after=None):
+            return keep.tile(shape, dtype, name=name, tag=after or name, align_bytes=64)
+
+        def load_list(name, source):
+            tile = lists.tile([P, S // GROUP], U16, name=name)
+            nc.sync.dma_start(tile[:], source)
+            return tile
 
         def multiply(acc, lhs_words, lhs_scales, rhs_words, rhs_scales):
             nc.tensor.matmul_mx(
@@ -62,163 +69,190 @@ def tile_picked_ccmpsoftbnorm2_none_p_kernel(
                 stop=True,
             )
 
+        offs_list = load_list("offs_list", offs)
+        w_rows = w1.rearrange("(p j) c -> p j c", j=PACK)
+        w_raw = [sbuf("w_raw%d" % h, [P, PACK, H // 2], F32) for h in range(2)]
+        nc.sync.dma_start(w_raw[0][:], w_rows[:, :, 0 : H // 2])
         table_scales = sbuf("table_scales", [P, T], U8)
         nc.vector.memset(table_scales[:].bitcast(I32), 0)
-        for q in range(4):
-            nc.scalar.dma_start(
+        for q in range(QUADRANTS):
+            nc.sync.dma_start(
                 table_scales[32 * q : 32 * q + 4, :].bitcast(I32),
                 x_scales[0, 4 * q : 4 * q + 4, :].bitcast(I32),
             )
+
         warm = sbuf("warm", [P, 16], F32)
         nc.vector.memset(warm[:, 0:8], 1.0)
         nc.scalar.activation(warm[:, 8:16], warm[:, 0:8], ACT.Abs_reciprocal_sqrt)
-        offs_list = load_list("offs_list", offs)
+
         cb_list = load_list("cb_list", cb)
-        w_rows = w1.rearrange("(p j) c -> p j c", j=PACK)
-        w_raw = []
-        for h in range(2):
-            piece = sbuf("w_raw%d" % h, [P, PACK, H // 2], F32)
-            nc.sync.dma_start(piece[:], w_rows[:, :, h * H // 2 : (h + 1) * H // 2])
-            w_raw.append(piece)
+        nc.sync.dma_start(w_raw[1][:], w_rows[:, :, H // 2 : H])
         table_words = sbuf("table_words", [P, T], U32)
-        nc.sync.dma_start(
-            table_words[:].bitcast(I32), x_words[0].rearrange("p n r -> p (n r)").bitcast(I32)
-        )
+        nc.sync.dma_start(table_words[:].bitcast(I32), x_words[0].rearrange("p n r -> p (n r)").bitcast(I32))
         n2_list = load_list("n2_list", n2)
         n1_list = load_list("n1_list", n1)
         ca_list = load_list("ca_list", ca)
         n4_list = load_list("n4_list", n4)
         n3_list = load_list("n3_list", n3)
         gain = sbuf("gain", [P, PACK], F32)
-        nc.gpsimd.dma_start(gain[:], gs.rearrange("(p t) o -> p (t o)", t=PACK))
+        nc.sync.dma_start(gain[:], gs.rearrange("(p t) o -> p (t o)", t=PACK))
 
-        def gather_scales(name, picks, tag):
-            tile = sbuf(name, [P, S], U8, tag)
-            nc.vector.tensor_copy(tile[:], table_scales[:].indirect(picks[:]))
+        def gather_scales(name, list_tile, after=None):
+            tile = sbuf(name, [P, S], U8, after)
+            nc.vector.tensor_copy(tile[:], table_scales[:].indirect(list_tile[:]))
             return tile
 
-        def gather_words(name, picks, tag):
-            tile = sbuf(name, [P, S], U32, tag)
-            nc.vector.tensor_copy(tile[:], table_words[:].indirect(picks[:]))
-            return tile
-
-        def deal(name, picked, dtype, run, tag):
-            tile = sbuf(name, [P, C], dtype, tag)
-            dst = tile[:].bitcast(I32) if dtype == U32 else tile[:]
-            src = picked.bitcast(I32) if dtype == U32 else picked
+        def deal(dealt, picked, run):
             nc.vector.tensor_copy(
-                dst.rearrange("p (t c i) -> p c t i", t=PACK, i=run),
-                src.rearrange("p (c i t) -> p c t i", t=PACK, i=run),
+                dealt.rearrange("p (t c i) -> p c t i", t=PACK, i=run),
+                picked.rearrange("p (c i t) -> p c t i", t=PACK, i=run),
             )
+
+        def deal_words(name, picked, after):
+            tile = sbuf(name, [P, C], U32, after)
+            deal(tile[:].bitcast(I32), picked.bitcast(I32), 4)
             return tile
 
-        token_scales = gather_scales("token_scales", offs_list, "token_scales")
-        cb_scales_picked = gather_scales("cb_scales_picked", cb_list, "cb_scales_picked")
+        def deal_scales(name, picked, after):
+            tile = sbuf(name, [P, C], U8, after)
+            deal(tile[:], picked, 16)
+            return tile
+
+        token_scales = gather_scales("token_scales", offs_list)
+        cb_scales_picked = gather_scales("cb_scales_picked", cb_list)
 
         w_bf = sbuf("w_bf", [P, PACK, P, PACK], BF16)
-        w_dst = w_bf[:].rearrange("p t m j -> p m t j")
+        w_dealt = w_bf[:].rearrange("p t m j -> p m t j")
         for h in range(2):
             nc.scalar.copy(
-                w_dst[:, h * P // 2 : (h + 1) * P // 2], w_raw[h][:].rearrange("p j (m t) -> p m t j", t=PACK)
+                w_dealt[:, h * P // 2 : (h + 1) * P // 2], w_raw[h][:].rearrange("p j (m t) -> p m t j", t=PACK)
             )
         w_words = sbuf("w_words", [P, H], U32)
         w_scales = sbuf("w_scales", [P, H], U8)
         nc.vector.quantize_mx(
             out=w_words[:].bitcast(FP8X4), scales=w_scales[:], in_=w_bf[:].rearrange("p t m j -> p (t m j)")
         )
-        early_words = sbuf("early_words", [P, 2, S], U32, "w_bf")
-        token_words = early_words[:, 0]
-        cb_words_picked = early_words[:, 1]
+
+        early_words = sbuf("early_words", [P, 2 * S], U32, "w_bf")
+        token_words = early_words[:, 0:S]
+        cb_words_picked = early_words[:, S : 2 * S]
         for h in range(2):
-            nc.vector.tensor_copy(token_words[:, half(h)], table_words[:].indirect(list_half(offs_list, h)))
-        y_psum = [bank(t, [P, S]) for t in range(PACK)]
-        for u in range(2):
-            for h, t in [(0, 2 * u), (0, 2 * u + 1), (1, 2 * u), (1, 2 * u + 1)]:
-                multiply(
-                    y_psum[t][:, half(h)],
-                    w_words[:, block(t)],
-                    w_scales[:, block(t)],
-                    token_words[:, half(h)],
-                    token_scales[:, half(h)],
-                )
+            nc.vector.tensor_copy(token_words[:, half(h)], table_words[:].indirect(entries(offs_list, half(h))))
+
+        y_psum = {t: bank(t, S) for t in range(1, PACK)}
+        y_halves = {(t, h): y_psum[t][:, half(h)] for t in range(1, PACK) for h in range(2)}
+        y_halves[(0, 0)] = bank(0, HALF)[:]
+        y_halves[(0, 1)] = bank(PACK, HALF)[:]
+        for pair in (WHOLE_TILES, SPLIT_TILES):
+            for h in range(2):
+                for t in pair:
+                    multiply(
+                        y_halves[(t, h)],
+                        w_words[:, block(t)],
+                        w_scales[:, block(t)],
+                        token_words[:, half(h)],
+                        token_scales[:, half(h)],
+                    )
         nc.vector.tensor_copy(cb_words_picked, table_words[:].indirect(cb_list[:]))
 
-        y_rows = [sbuf("y_rows%d" % t, [P, S + SPARE], F32) for t in range(PACK)]
-        y_size = [sbuf("y_size%d" % t, [P, S + SPARE], F32) for t in range(PACK)]
-        for t in range(PACK):
+        widths = [S + SPARE if t in WHOLE_TILES else S for t in range(PACK)]
+        y_rows = [sbuf("y_rows%d" % t, [P, widths[t]], F32) for t in range(PACK)]
+        y_size = [sbuf("y_size%d" % t, [P, widths[t]], F32) for t in range(PACK)]
+        for t in WHOLE_TILES:
             nc.gpsimd.memset(y_rows[t][:, S : S + SPARE], 0.0)
             nc.gpsimd.memset(y_size[t][:, S : S + SPARE], 0.0)
-        root = sbuf("root", [P, 2, PACK, HALF], F32)
-        part = sbuf("part", [P, 2, PACK, HALF], F32)
-        z_words = sbuf("z_words", [P, S], U32)
-        z_scales = sbuf("z_scales", [P, S], U8)
-        denom = {}
-
-        upper = {}
-        other = {}
-
-        def span(h0, h1):
-            return slice(h0 * HALF, h1 * HALF)
-
-        def picks_of(tile, h0, h1):
-            return tile[:, h0 * HALF // 16 : h1 * HALF // 16]
-
-        def copy_y(t):
-            nc.vector.tensor_copy(y_rows[t][:, 0:S], y_psum[t][:])
-
-        def size_on_scalar(t):
-            nc.scalar.activation(y_size[t][:, 0:S], y_psum[t][:], ACT.Abs)
 
         def size_on_vector(t):
             nc.vector.scalar_tensor_tensor(y_size[t][:, 0:S], y_psum[t][:], -1.0, y_rows[t][:, 0:S], ALU.mult, ALU.max)
 
-        def fetch_other(t, h0, h1, tag=None):
-            other[(t, h0)] = sbuf("other%d_%d" % (t, h0), [P, (h1 - h0) * HALF], F32, tag)
-            nc.scalar.activation(other[(t, h0)][:], y_size[t][:].indirect(picks_of(n2_list, h0, h1)), ACT.Copy)
+        for h in range(2):
+            nc.scalar.activation(y_size[0][:, half(h)], y_halves[(0, h)], ACT.Abs)
+        for h in range(2):
+            nc.vector.tensor_copy(y_rows[0][:, half(h)], y_halves[(0, h)])
+        for t in range(1, PACK):
+            nc.vector.tensor_copy(y_rows[t][:, 0:S], y_psum[t][:])
+            if t > 1:
+                size_on_vector(t - 1)
+        size_on_vector(PACK - 1)
 
-        def fetch_upper(t, h0, h1, tag=None):
-            upper[(t, h0)] = sbuf("upper%d_%d" % (t, h0), [P, (h1 - h0) * HALF], F32, tag)
-            nc.scalar.activation(upper[(t, h0)][:], y_rows[t][:].indirect(picks_of(n1_list, h0, h1)), ACT.Copy)
+        root = sbuf("root", [P, 2, PACK, HALF], F32)
+        part = sbuf("part", [P, 2, PACK, HALF], F32)
+        z_words = sbuf("z_words", [P, S], U32)
+        z_scales = sbuf("z_scales", [P, S], U8)
+        upper, other, denom, z_bf = {}, {}, {}, {}
 
-        def add_sizes(t, h0, h1):
-            denom[(t, h0)] = sbuf("denom%d_%d" % (t, h0), [P, (h1 - h0) * HALF], F32)
-            nc.vector.scalar_tensor_tensor(
-                denom[(t, h0)][:], other[(t, h0)][:], 0.5, y_size[t][:, span(h0, h1)], ALU.add, ALU.add
-            )
+        def piece_tile(kind, piece, after=None):
+            t, h0, h1 = piece
+            return sbuf("%s%d_%d" % (kind, t, h0), [P, (h1 - h0) * HALF], F32, after)
 
-        def take_root(t, h0, h1):
+        def fetch_other(piece, after=None):
+            t, h0, h1 = piece
+            other[piece] = piece_tile("other", piece, after)
+            nc.scalar.activation(other[piece][:], y_size[t][:].indirect(entries(n2_list, halves(h0, h1))), ACT.Copy)
+
+        def fetch_upper(piece, after=None):
+            t, h0, h1 = piece
+            upper[piece] = piece_tile("upper", piece, after)
+            nc.scalar.activation(upper[piece][:], y_rows[t][:].indirect(entries(n1_list, halves(h0, h1))), ACT.Copy)
+
+        def add_sizes(piece):
+            t, h0, h1 = piece
+            denom[piece] = piece_tile("denom", piece)
+            nc.vector.tensor_tensor(denom[piece][:], other[piece][:], y_size[t][:, halves(h0, h1)], ALU.add)
+
+        def take_root(piece):
+            t, h0, h1 = piece
             nc.scalar.activation(
-                root[:, h0:h1, t], denom[(t, h0)][:].rearrange("p (h c) -> p h c", c=HALF), ACT.Abs_reciprocal_sqrt
+                root[:, h0:h1, t],
+                denom[piece][:].rearrange("p (h c) -> p h c", c=HALF),
+                ACT.Abs_reciprocal_sqrt,
+                bias=0.5,
             )
 
-        def first_product(t, h0, h1):
+        def first_product(piece):
+            t, h0, h1 = piece
             nc.vector.scalar_tensor_tensor(
                 part[:, h0:h1, t],
-                upper[(t, h0)][:].rearrange("p (h c) -> p h c", c=HALF),
+                upper[piece][:].rearrange("p (h c) -> p h c", c=HALF),
                 gain[:, t : t + 1],
                 root[:, h0:h1, t],
                 ALU.mult,
                 ALU.mult,
             )
 
-        z_planes = {}
-
         def second_product(h):
-            z_bf = sbuf("z_bf%d" % h, [P, HALF * PACK], BF16)
+            z_bf[h] = sbuf("z_bf%d" % h, [P, HALF * PACK], BF16)
             nc.vector.tensor_tensor(
-                z_bf[:].rearrange("p (c i t) -> p c t i", i=2, t=PACK),
+                z_bf[h][:].rearrange("p (c i t) -> p c t i", i=2, t=PACK),
                 part[:, h].rearrange("p t (c i) -> p c t i", i=2),
                 root[:, h].rearrange("p t (c i) -> p c t i", i=2),
                 ALU.mult,
             )
-            z_planes[h] = z_bf
 
         def quantise_z(h):
-            nc.vector.quantize_mx(
-                out=z_words[:, half(h)].bitcast(FP8X4), scales=z_scales[:, half(h)], in_=z_planes[h][:]
-            )
+            nc.vector.quantize_mx(out=z_words[:, half(h)].bitcast(FP8X4), scales=z_scales[:, half(h)], in_=z_bf[h][:])
 
-        b_psum = [bank(PACK + t, [P, S]) for t in range(PACK)]
+        whole = [(t, 0, 2) for t in WHOLE_TILES]
+        early = [(t, 0, 1) for t in SPLIT_TILES]
+        late = [(t, 1, 2) for t in SPLIT_TILES]
+        for piece in whole:
+            fetch_other(piece)
+            fetch_upper(piece)
+        for piece in early:
+            fetch_other(piece)
+        for piece in early:
+            fetch_upper(piece)
+        cb_words = deal_words("cb_words", cb_words_picked, "w_words")
+        cb_scales = deal_scales("cb_scales", cb_scales_picked[:], "w_scales")
+        ca_scales_picked = gather_scales("ca_scales_picked", ca_list, "token_scales")
+        for piece in whole + early:
+            add_sizes(piece)
+        for piece in whole + early:
+            take_root(piece)
+            first_product(piece)
+        second_product(0)
+
+        b_psum = [bank(PACK + t, S) for t in range(PACK)]
 
         def score_b(h):
             for t in range(PACK):
@@ -230,108 +264,61 @@ def tile_picked_ccmpsoftbnorm2_none_p_kernel(
                     z_scales[:, half(h)],
                 )
 
-        size_on_scalar(0)
-        copy_y(0)
-        copy_y(1)
-        copy_y(2)
-        size_on_vector(1)
-        copy_y(3)
-        size_on_vector(2)
-        size_on_vector(3)
-        fetch_other(0, 0, 2)
-        fetch_upper(0, 0, 2)
-        fetch_other(1, 0, 2)
-        fetch_upper(1, 0, 2)
-        fetch_other(2, 0, 1)
-        fetch_other(3, 0, 1)
-        fetch_upper(2, 0, 1)
-        fetch_upper(3, 0, 1)
-        cb_words = deal("cb_words", cb_words_picked, U32, 4, "w_words")
-        cb_scales = deal("cb_scales", cb_scales_picked[:], U8, 16, "w_scales")
-        ca_scales_picked = gather_scales("ca_scales_picked", ca_list, "token_scales")
-        add_sizes(0, 0, 2)
-        add_sizes(1, 0, 2)
-        add_sizes(2, 0, 1)
-        add_sizes(3, 0, 1)
-        ca_scales = deal("ca_scales", ca_scales_picked[:], U8, 16, "ca_scales")
-        take_root(0, 0, 2)
-        first_product(0, 0, 2)
-        take_root(1, 0, 2)
-        first_product(1, 0, 2)
-        take_root(2, 0, 1)
-        first_product(2, 0, 1)
-        take_root(3, 0, 1)
-        first_product(3, 0, 1)
-        second_product(0)
-        fetch_other(2, 1, 2, "denom2_0")
-        fetch_other(3, 1, 2, "denom3_0")
-        add_sizes(2, 1, 2)
-        add_sizes(3, 1, 2)
+        for piece in late:
+            fetch_other(piece, "denom%d_0" % piece[0])
+        for piece in late:
+            add_sizes(piece)
         quantise_z(0)
         score_b(0)
-        fetch_upper(2, 1, 2, "upper2_0")
-        take_root(2, 1, 2)
-        take_root(3, 1, 2)
-        fetch_upper(3, 1, 2, "upper3_0")
-        first_product(2, 1, 2)
-        first_product(3, 1, 2)
+        for piece in late:
+            fetch_upper(piece, "upper%d_0" % piece[0])
+        for piece in late:
+            take_root(piece)
+        for piece in late:
+            first_product(piece)
         second_product(1)
         quantise_z(1)
 
-        spent = ["denom3_1","upper3_0","part","root"]
+        spent = ["denom3_1", "upper3_0", "part", "root"]
         b_window = [sbuf("b_window%d" % t, [P, 2 * S], F32, spent[t]) for t in range(PACK)]
         a_window = [sbuf("a_window%d" % t, [P, 2 * S], F32) for t in range(PACK)]
-        gated = {}
-        a_psum = {}
-        out_rows = out.rearrange("(p t) j -> t p j", t=PACK)
+        gate = [b_window[t][:, S : 2 * S] for t in range(PACK)]
+        b_picked = [a_window[t][:, S : 2 * S] for t in range(PACK)]
 
         def take_tanh(h):
             for t in range(PACK):
-                nc.scalar.activation(
-                    b_window[t][:, S + h * HALF : S + (h + 1) * HALF], b_psum[t][:, half(h)], ACT.Tanh, scale=0.0625
-                )
-
-        def copy_b(t):
-            nc.vector.tensor_scalar(b_window[t][:, 0:S], b_psum[t][:], 0.0625, None, ALU.mult)
-
-        def fetch_b(t):
-            nc.scalar.activation(a_window[t][:, S : 2 * S], b_window[t][:].indirect(n4_list[:]), ACT.Copy)
-
-        def score_a():
-            for t in range(PACK):
-                a_psum[t] = bank(t, [P, S])
-                multiply(a_psum[t][:], ca_words[:, block(t)], ca_scales[:, block(t)], z_words[:], z_scales[:])
-
-        def copy_a(t):
-            nc.vector.tensor_scalar(a_window[t][:, 0:S], a_psum[t][:], 0.0625, None, ALU.mult)
-
-        def apply_gate(t):
-            gated[t] = sbuf("gated%d" % t, [P, S], F32)
-            nc.vector.tensor_tensor(gated[t][:], a_window[t][:, S : 2 * S], b_window[t][:, S : 2 * S], ALU.mult)
-
-        def finish(t, pieces):
-            a_picked = sbuf("a_picked%d" % t, [P, S], F32)
-            result = sbuf("result%d" % t, [P, S], F32)
-            width = S // pieces
-            for piece in range(pieces):
-                cols = slice(piece * width, (piece + 1) * width)
-                picks = n3_list[:, piece * width // 16 : (piece + 1) * width // 16]
-                nc.scalar.activation(a_picked[:, cols], a_window[t][:].indirect(picks), ACT.Copy)
-                nc.vector.tensor_tensor(result[:, cols], a_picked[:, cols], gated[t][:, cols], ALU.subtract)
-                nc.sync.dma_start(out_rows[t][:, cols], result[:, cols])
+                nc.scalar.activation(gate[t][:, half(h)], b_psum[t][:, half(h)], ACT.Tanh, scale=SCORE_SCALE)
 
         take_tanh(0)
         score_b(1)
         take_tanh(1)
-        ca_words_picked = gather_words("ca_words_picked", ca_list, "z_bf1")
-        ca_words = deal("ca_words", ca_words_picked[:], U32, 4, "w_words")
-        for t in range(PACK):
-            copy_b(t)
+
+        def fetch_b(t):
+            nc.vector.tensor_scalar(b_window[t][:, 0:S], b_psum[t][:], SCORE_SCALE, None, ALU.mult)
+            nc.scalar.activation(b_picked[t], b_window[t][:].indirect(n4_list[:]), ACT.Copy)
+
+        ca_words_picked = sbuf("ca_words_picked", [P, S], U32, "z_bf1")
+        nc.vector.tensor_copy(ca_words_picked[:], table_words[:].indirect(ca_list[:]))
+        for t in range(PACK // 2):
             fetch_b(t)
-        score_a()
+        ca_words = deal_words("ca_words", ca_words_picked[:], "w_words")
+        ca_scales = deal_scales("ca_scales", ca_scales_picked[:], "w_scales")
+        for t in range(PACK // 2, PACK):
+            fetch_b(t)
+        a_psum = [bank(t, S) for t in range(PACK)]
         for t in range(PACK):
-            copy_a(t)
+            multiply(a_psum[t][:], ca_words[:, block(t)], ca_scales[:, block(t)], z_words[:], z_scales[:])
         for t in range(PACK):
-            apply_gate(t)
+            nc.vector.tensor_scalar(a_window[t][:, 0:S], a_psum[t][:], SCORE_SCALE, None, ALU.mult)
+        gated = [sbuf("gated%d" % t, [P, S], F32) for t in range(PACK)]
         for t in range(PACK):
-            finish(t, 2 if t == PACK - 1 else 1)
+            nc.vector.tensor_tensor(gated[t][:], b_picked[t], gate[t], ALU.mult)
+
+        out_rows = out.rearrange("(p t) j -> t p j", t=PACK)
+        for t in range(PACK):
+            a_picked = sbuf("a_picked%d" % t, [P, S], F32)
+            result = sbuf("result%d" % t, [P, S], F32)
+            for cols in [half(0), half(1)] if t == PACK - 1 else [halves(0, 2)]:
+                nc.scalar.activation(a_picked[:, cols], a_window[t][:].indirect(entries(n3_list, cols)), ACT.Copy)
+                nc.vector.tensor_tensor(result[:, cols], a_picked[:, cols], gated[t][:, cols], ALU.subtract)
+                nc.sync.dma_start(out_rows[t][:, cols], result[:, cols])

from contextlib import ExitStack

import concourse.mybir as mybir

K, T, S, H, C = 512, 2048, 512, 512, 512
FLOPS = 2 * K * H * S + 2 * 2 * K * C * S

F32 = mybir.dt.float32
BF16 = mybir.dt.bfloat16
I32 = mybir.dt.int32
U32 = mybir.dt.uint32
U16 = mybir.dt.uint16
U8 = mybir.dt.uint8
FP8X4 = mybir.dt.float8_e4m3fn_x4
ALU = mybir.AluOpType
ACT = mybir.ActivationFunctionType

P = 128
PACK = 4
GROUP = 16
QUADRANTS = 4
HALF = S // 2
SPARE = 8
SCORE_SCALE = 0.0625
WHOLE_TILES = (0, 1)
SPLIT_TILES = (2, 3)


def tile_picked_ccmpsoftbnorm2_none_p_kernel(
    tc, x_words, x_scales, w1, gs, offs, n1, n2, ca, cb, n3, n4, out
):
    nc = tc.nc
    with ExitStack() as ctx:
        lists = ctx.enter_context(tc.tile_pool(name="lists", bufs=1))
        keep = ctx.enter_context(tc.tile_pool(name="keep", bufs=1))
        psum = ctx.enter_context(tc.psum_pool(name="psum", bufs=1))

        def halves(h0, h1):
            return slice(h0 * HALF, h1 * HALF)

        def half(h):
            return halves(h, h + 1)

        def entries(list_tile, cols):
            return list_tile[:, cols.start // GROUP : cols.stop // GROUP]

        def block(t):
            return slice(t * P, (t + 1) * P)

        def bank(index, width):
            return psum.tile([P, width], F32, name="bank%d" % index)

        def sbuf(name, shape, dtype, after=None):
            return keep.tile(shape, dtype, name=name, tag=after or name, align_bytes=64)

        def load_list(name, source):
            tile = lists.tile([P, S // GROUP], U16, name=name)
            nc.sync.dma_start(tile[:], source)
            return tile

        def multiply(acc, lhs_words, lhs_scales, rhs_words, rhs_scales):
            nc.tensor.matmul_mx(
                out=acc,
                lhsT=lhs_words.bitcast(FP8X4),
                lhsT_scale=lhs_scales,
                rhs=rhs_words.bitcast(FP8X4),
                rhs_scale=rhs_scales,
                start=True,
                stop=True,
            )

        offs_list = load_list("offs_list", offs)
        w_rows = w1.rearrange("(p j) c -> p j c", j=PACK)
        w_raw = [sbuf("w_raw%d" % h, [P, PACK, H // 2], F32) for h in range(2)]
        nc.sync.dma_start(w_raw[0][:], w_rows[:, :, 0 : H // 2])
        table_scales = sbuf("table_scales", [P, T], U8)
        nc.vector.memset(table_scales[:].bitcast(I32), 0)
        for q in range(QUADRANTS):
            nc.sync.dma_start(
                table_scales[32 * q : 32 * q + 4, :].bitcast(I32),
                x_scales[0, 4 * q : 4 * q + 4, :].bitcast(I32),
            )

        warm = sbuf("warm", [P, 16], F32)
        nc.vector.memset(warm[:, 0:8], 1.0)
        nc.scalar.activation(warm[:, 8:16], warm[:, 0:8], ACT.Abs_reciprocal_sqrt)

        cb_list = load_list("cb_list", cb)
        nc.sync.dma_start(w_raw[1][:], w_rows[:, :, H // 2 : H])
        table_words = sbuf("table_words", [P, T], U32)
        nc.sync.dma_start(table_words[:].bitcast(I32), x_words[0].rearrange("p n r -> p (n r)").bitcast(I32))
        n2_list = load_list("n2_list", n2)
        n1_list = load_list("n1_list", n1)
        ca_list = load_list("ca_list", ca)
        n4_list = load_list("n4_list", n4)
        n3_list = load_list("n3_list", n3)
        gain = sbuf("gain", [P, PACK], F32)
        nc.sync.dma_start(gain[:], gs.rearrange("(p t) o -> p (t o)", t=PACK))

        def gather_scales(name, list_tile, after=None):
            tile = sbuf(name, [P, S], U8, after)
            nc.vector.tensor_copy(tile[:], table_scales[:].indirect(list_tile[:]))
            return tile

        def deal(dealt, picked, run):
            nc.vector.tensor_copy(
                dealt.rearrange("p (t c i) -> p c t i", t=PACK, i=run),
                picked.rearrange("p (c i t) -> p c t i", t=PACK, i=run),
            )

        def deal_words(name, picked, after):
            tile = sbuf(name, [P, C], U32, after)
            deal(tile[:].bitcast(I32), picked.bitcast(I32), 4)
            return tile

        def deal_scales(name, picked, after):
            tile = sbuf(name, [P, C], U8, after)
            deal(tile[:], picked, 16)
            return tile

        token_scales = gather_scales("token_scales", offs_list)
        cb_scales_picked = gather_scales("cb_scales_picked", cb_list)

        w_bf = sbuf("w_bf", [P, PACK, P, PACK], BF16)
        w_dealt = w_bf[:].rearrange("p t m j -> p m t j")
        for h in range(2):
            nc.scalar.copy(
                w_dealt[:, h * P // 2 : (h + 1) * P // 2], w_raw[h][:].rearrange("p j (m t) -> p m t j", t=PACK)
            )
        w_words = sbuf("w_words", [P, H], U32)
        w_scales = sbuf("w_scales", [P, H], U8)
        nc.vector.quantize_mx(
            out=w_words[:].bitcast(FP8X4), scales=w_scales[:], in_=w_bf[:].rearrange("p t m j -> p (t m j)")
        )

        early_words = sbuf("early_words", [P, 2 * S], U32, "w_bf")
        token_words = early_words[:, 0:S]
        cb_words_picked = early_words[:, S : 2 * S]
        for h in range(2):
            nc.vector.tensor_copy(token_words[:, half(h)], table_words[:].indirect(entries(offs_list, half(h))))

        y_psum = {t: bank(t, S) for t in range(1, PACK)}
        y_halves = {(t, h): y_psum[t][:, half(h)] for t in range(1, PACK) for h in range(2)}
        y_halves[(0, 0)] = bank(0, HALF)[:]
        y_halves[(0, 1)] = bank(PACK, HALF)[:]
        for pair in (WHOLE_TILES, SPLIT_TILES):
            for h in range(2):
                for t in pair:
                    multiply(
                        y_halves[(t, h)],
                        w_words[:, block(t)],
                        w_scales[:, block(t)],
                        token_words[:, half(h)],
                        token_scales[:, half(h)],
                    )
        nc.vector.tensor_copy(cb_words_picked, table_words[:].indirect(cb_list[:]))

        widths = [S + SPARE if t in WHOLE_TILES else S for t in range(PACK)]
        y_rows = [sbuf("y_rows%d" % t, [P, widths[t]], F32) for t in range(PACK)]
        y_size = [sbuf("y_size%d" % t, [P, widths[t]], F32) for t in range(PACK)]
        for t in WHOLE_TILES:
            nc.gpsimd.memset(y_rows[t][:, S : S + SPARE], 0.0)
            nc.gpsimd.memset(y_size[t][:, S : S + SPARE], 0.0)

        def size_on_vector(t):
            nc.vector.scalar_tensor_tensor(y_size[t][:, 0:S], y_psum[t][:], -1.0, y_rows[t][:, 0:S], ALU.mult, ALU.max)

        for h in range(2):
            nc.scalar.activation(y_size[0][:, half(h)], y_halves[(0, h)], ACT.Abs)
        for h in range(2):
            nc.vector.tensor_copy(y_rows[0][:, half(h)], y_halves[(0, h)])
        for t in range(1, PACK):
            nc.vector.tensor_copy(y_rows[t][:, 0:S], y_psum[t][:])
            if t > 1:
                size_on_vector(t - 1)
        size_on_vector(PACK - 1)

        root = sbuf("root", [P, 2, PACK, HALF], F32)
        part = sbuf("part", [P, 2, PACK, HALF], F32)
        z_words = sbuf("z_words", [P, S], U32)
        z_scales = sbuf("z_scales", [P, S], U8)
        upper, other, denom, z_bf = {}, {}, {}, {}

        def piece_tile(kind, piece, after=None):
            t, h0, h1 = piece
            return sbuf("%s%d_%d" % (kind, t, h0), [P, (h1 - h0) * HALF], F32, after)

        def fetch_other(piece, after=None):
            t, h0, h1 = piece
            other[piece] = piece_tile("other", piece, after)
            nc.scalar.activation(other[piece][:], y_size[t][:].indirect(entries(n2_list, halves(h0, h1))), ACT.Copy)

        def fetch_upper(piece, after=None):
            t, h0, h1 = piece
            upper[piece] = piece_tile("upper", piece, after)
            nc.scalar.activation(upper[piece][:], y_rows[t][:].indirect(entries(n1_list, halves(h0, h1))), ACT.Copy)

        def add_sizes(piece):
            t, h0, h1 = piece
            denom[piece] = piece_tile("denom", piece)
            nc.vector.tensor_tensor(denom[piece][:], other[piece][:], y_size[t][:, halves(h0, h1)], ALU.add)

        def take_root(piece):
            t, h0, h1 = piece
            nc.scalar.activation(
                root[:, h0:h1, t],
                denom[piece][:].rearrange("p (h c) -> p h c", c=HALF),
                ACT.Abs_reciprocal_sqrt,
                bias=0.5,
            )

        def first_product(piece):
            t, h0, h1 = piece
            nc.vector.scalar_tensor_tensor(
                part[:, h0:h1, t],
                upper[piece][:].rearrange("p (h c) -> p h c", c=HALF),
                gain[:, t : t + 1],
                root[:, h0:h1, t],
                ALU.mult,
                ALU.mult,
            )

        def second_product(h):
            z_bf[h] = sbuf("z_bf%d" % h, [P, HALF * PACK], BF16)
            nc.vector.tensor_tensor(
                z_bf[h][:].rearrange("p (c i t) -> p c t i", i=2, t=PACK),
                part[:, h].rearrange("p t (c i) -> p c t i", i=2),
                root[:, h].rearrange("p t (c i) -> p c t i", i=2),
                ALU.mult,
            )

        def quantise_z(h):
            nc.vector.quantize_mx(out=z_words[:, half(h)].bitcast(FP8X4), scales=z_scales[:, half(h)], in_=z_bf[h][:])

        whole = [(t, 0, 2) for t in WHOLE_TILES]
        early = [(t, 0, 1) for t in SPLIT_TILES]
        late = [(t, 1, 2) for t in SPLIT_TILES]
        for piece in whole:
            fetch_other(piece)
            fetch_upper(piece)
        for piece in early:
            fetch_other(piece)
        for piece in early:
            fetch_upper(piece)
        cb_words = deal_words("cb_words", cb_words_picked, "w_words")
        cb_scales = deal_scales("cb_scales", cb_scales_picked[:], "w_scales")
        ca_scales_picked = gather_scales("ca_scales_picked", ca_list, "token_scales")
        for piece in whole + early:
            add_sizes(piece)
        for piece in whole + early:
            take_root(piece)
            first_product(piece)
        second_product(0)

        b_psum = [bank(PACK + t, S) for t in range(PACK)]

        def score_b(h):
            for t in range(PACK):
                multiply(
                    b_psum[t][:, half(h)],
                    cb_words[:, block(t)],
                    cb_scales[:, block(t)],
                    z_words[:, half(h)],
                    z_scales[:, half(h)],
                )

        for piece in late:
            fetch_other(piece, "denom%d_0" % piece[0])
        for piece in late:
            add_sizes(piece)
        quantise_z(0)
        score_b(0)
        for piece in late:
            fetch_upper(piece, "upper%d_0" % piece[0])
        for piece in late:
            take_root(piece)
        for piece in late:
            first_product(piece)
        second_product(1)
        quantise_z(1)

        spent = ["denom3_1", "upper3_0", "part", "root"]
        b_window = [sbuf("b_window%d" % t, [P, 2 * S], F32, spent[t]) for t in range(PACK)]
        a_window = [sbuf("a_window%d" % t, [P, 2 * S], F32) for t in range(PACK)]
        gate = [b_window[t][:, S : 2 * S] for t in range(PACK)]
        b_picked = [a_window[t][:, S : 2 * S] for t in range(PACK)]

        def take_tanh(h):
            for t in range(PACK):
                nc.scalar.activation(gate[t][:, half(h)], b_psum[t][:, half(h)], ACT.Tanh, scale=SCORE_SCALE)

        take_tanh(0)
        score_b(1)
        take_tanh(1)

        def fetch_b(t):
            nc.vector.tensor_scalar(b_window[t][:, 0:S], b_psum[t][:], SCORE_SCALE, None, ALU.mult)
            nc.scalar.activation(b_picked[t], b_window[t][:].indirect(n4_list[:]), ACT.Copy)

        ca_words_picked = sbuf("ca_words_picked", [P, S], U32, "z_bf1")
        nc.vector.tensor_copy(ca_words_picked[:], table_words[:].indirect(ca_list[:]))
        for t in range(PACK // 2):
            fetch_b(t)
        ca_words = deal_words("ca_words", ca_words_picked[:], "w_words")
        ca_scales = deal_scales("ca_scales", ca_scales_picked[:], "w_scales")
        for t in range(PACK // 2, PACK):
            fetch_b(t)
        a_psum = [bank(t, S) for t in range(PACK)]
        for t in range(PACK):
            multiply(a_psum[t][:], ca_words[:, block(t)], ca_scales[:, block(t)], z_words[:], z_scales[:])
        for t in range(PACK):
            nc.vector.tensor_scalar(a_window[t][:, 0:S], a_psum[t][:], SCORE_SCALE, None, ALU.mult)
        gated = [sbuf("gated%d" % t, [P, S], F32) for t in range(PACK)]
        for t in range(PACK):
            nc.vector.tensor_tensor(gated[t][:], b_picked[t], gate[t], ALU.mult)

        out_rows = out.rearrange("(p t) j -> t p j", t=PACK)
        for t in range(PACK):
            a_picked = sbuf("a_picked%d" % t, [P, S], F32)
            result = sbuf("result%d" % t, [P, S], F32)
            for cols in [half(0), half(1)] if t == PACK - 1 else [halves(0, 2)]:
                nc.scalar.activation(a_picked[:, cols], a_window[t][:].indirect(entries(n3_list, cols)), ACT.Copy)
                nc.vector.tensor_tensor(result[:, cols], a_picked[:, cols], gated[t][:, cols], ALU.subtract)
                nc.sync.dma_start(out_rows[t][:, cols], result[:, cols])
